import numpy as np
import ml_dtypes


def mxq(x, axis, fmt="e4m3"):
    dtype, down = {"e4m3": (ml_dtypes.float8_e4m3fn, 7), "e5m2": (ml_dtypes.float8_e5m2, 14)}[fmt]
    v = np.moveaxis(np.asarray(x, np.float32).astype(ml_dtypes.bfloat16).astype(np.float64), axis, -1)
    blocks = v.reshape(v.shape[:-1] + (-1, 32))
    amax = np.abs(blocks).max(-1, keepdims=True)
    byte = np.maximum(np.where(amax > 0, np.frexp(amax)[1] - 1 + 127, 0) - down, 1)
    scale = np.exp2(byte - 127.0)
    codes = (blocks / scale).astype(np.float32).astype(dtype).astype(np.float64)
    return np.moveaxis((codes * scale).reshape(v.shape), -1, axis)


WIDE = False


def mx_kscale(k):
    if not WIDE:
        return np.ones(k)
    levels = np.array([30, -30])
    if k % 512:
        return np.exp2(np.random.permutation(np.resize(levels, k // 32))).repeat(32)
    a = np.empty((k // 512, 16))
    for p in range(k // 512):
        a[p, :8] = np.random.permutation(np.resize(levels, 8))
        for g in range(8):
            far = levels[np.abs(levels - a[p, g]) >= 10]
            a[p, g + 8] = far[np.random.randint(len(far))]
    return np.exp2(a.ravel()).repeat(32)


def f64(x):
    return np.asarray(x).astype(np.float64)


def striped(idx):
    return np.tile(np.asarray(idx).reshape(-1, 16).T, (8, 1)).astype(np.uint16)


def unstriped(offs):
    return offs[:16].T.reshape(-1).astype(np.int64)


E2M1 = np.array([0.0, 0.5, 1.0, 1.5, 2.0, 3.0, 4.0, 6.0, -0.0, -0.5, -1.0, -1.5, -2.0, -3.0, -4.0, -6.0])


def pack_weight(w, fmt):
    k, n = w.shape
    w = f64(np.asarray(w, np.float32).astype(ml_dtypes.bfloat16)).reshape(k // 32, 32, n)
    amax = np.abs(w).max(1)
    if fmt in ("e4m3", "e5m2"):
        byte = np.frexp(amax)[1] - 1 + 127 - (7 if fmt == "e4m3" else 14)
    else:
        mant, ex = np.frexp(amax / 6.0)
        byte = np.where(mant > 0.5, ex, ex - 1) + 127
    byte = np.clip(np.where(amax > 0, byte, 1), 1, 254)
    scaled = (w * np.exp2(127.0 - byte)[:, None, :]).reshape(k, n).astype(np.float32)
    by_word = np.ascontiguousarray(scaled.reshape(k // 512, 128, 4, n).transpose(0, 1, 3, 2))
    if fmt in ("e4m3", "e5m2"):
        words = by_word.astype(ml_dtypes.float8_e4m3fn if fmt == "e4m3" else ml_dtypes.float8_e5m2).view(np.uint8)
    else:
        c = by_word.astype(ml_dtypes.float4_e2m1fn).view(np.uint8) & 0xF
        words = (c[..., 0::2] | (c[..., 1::2] << 4)).reshape(k // 512, 128, 2 * n)
    return np.ascontiguousarray(words), np.ascontiguousarray(byte.astype(np.uint8).reshape(k // 512, 16, n))


def unpack_weight(words, scales, fmt):
    g, _, n = scales.shape
    words = np.ascontiguousarray(words).reshape(g, 128, n, -1)
    if fmt in ("e4m3", "e5m2"):
        vals = words.view(ml_dtypes.float8_e4m3fn if fmt == "e4m3" else ml_dtypes.float8_e5m2).astype(np.float64)
    else:
        nib = np.empty((g, 128, n, 4), np.uint8)
        nib[..., 0::2] = words & 0xF
        nib[..., 1::2] = words >> 4
        vals = E2M1[nib]
    vals = vals * np.repeat(np.exp2(scales.astype(np.float64) - 127.0), 8, axis=1)[..., None]
    return vals.transpose(0, 1, 3, 2).reshape(g * 512, n)


K, T, J, B, R, N = 512, 512, 128, 16, 512, 256


def setup_inputs():
    n = np.random.standard_normal
    idx = np.random.permutation(T)[:J]
    fk = mx_kscale(K)
    fr = mx_kscale(R)
    wp = pack_weight(n((K, R)) * 1 / np.sqrt(K) * fk[:, None] * fr, "e5m2")
    wbp = pack_weight(n((R, N)) * 1 / np.sqrt(R) / fr[:, None], "e2m1")
    return {
        "xf": (n((K, T))).astype(np.float32),
        "fk": (np.random.uniform(0.5, 2.0, (K, 1)) / fk[:, None]).astype(np.float32),
        "w_words": wp[0],
        "w_scales": wp[1],
        "us": (np.random.uniform(0.5, 2.0, (R, 1)) * fr[:, None]).astype(np.float32),
        "wb_words": wbp[0],
        "wb_scales": wbp[1],
        "rs": (1.0 * n((J, N))).astype(np.float32),
        "offs": striped(idx),
    }


def reference(xf, fk, w_words, w_scales, us, wb_words, wb_scales, rs, offs):
    idx = unstriped(offs)
    wu = unpack_weight(w_words, w_scales, "e5m2")
    wbu = unpack_weight(wb_words, wb_scales, "e2m1")
    xg = f64(xf)[:, idx]
    g1 = xg.reshape(K, B, J // B).mean(axis=2)
    g2 = np.repeat(g1, J // B, axis=1)
    u = (xg - g2) * f64(fk)
    uq = mxq(u, 0, "e5m2")
    a = wu.T @ uq
    pk1 = np.max(np.abs(a), axis=1, keepdims=True)
    hid = a / pk1 * f64(us)
    hidq = mxq(hid, 0, "e5m2")
    p = hidq.T @ wbu
    pk2 = np.max(np.abs(p), axis=1, keepdims=True)
    y = p / (pk2 + 0.2) + 0.3 * f64(rs)
    return y

@@ -1,0 +1,168 @@
+from contextlib import ExitStack
+
+import concourse.mybir as mybir
+
+K, T, J, B, R, N = 512, 512, 128, 16, 512, 256
+FLOPS = 2 * K * R * J + 2 * R * J * N
+
+F32 = mybir.dt.float32
+BF16 = mybir.dt.bfloat16
+I32 = mybir.dt.int32
+U32 = mybir.dt.uint32
+U16 = mybir.dt.uint16
+U8 = mybir.dt.uint8
+E5M2X4 = mybir.dt.float8_e5m2_x4
+E2M1X4 = mybir.dt.float4_e2m1fn_x4
+ALU = mybir.AluOpType
+ACT = mybir.ActivationFunctionType
+AXIS_X = mybir.AxisListType.X
+
+P = 128
+PACK = 4
+GROUP = J // B
+QUADRANTS = 4
+
+
+def load_scale_rows(queue, plane, scales):
+    rows = scales[0].bitcast(I32)
+    view = plane[:].bitcast(I32)
+    for q in range(QUADRANTS):
+        queue.dma_start(out=view[32 * q : 32 * q + 4, :], in_=rows[4 * q : 4 * q + 4, :])
+
+
+def load_scale_rows_repeated(queues, plane, scales):
+    rows = scales[0].bitcast(I32)
+    view = plane[:].bitcast(I32)
+    words = rows.shape[1]
+    for q in range(QUADRANTS):
+        queues[q].dma_start(
+            out=view[32 * q : 32 * q + 32, :],
+            in_=rows[4 * q : 4 * q + 4, :].unsqueeze(0).to_broadcast([8, 4, words]),
+        )
+
+
+def tile_list_centredpicks_peakscaled_rowpeaks_kernel(tc, xf, fk, w_words, w_scales, us, wb_words, wb_scales, rs, offs, out):
+    nc = tc.nc
+    with ExitStack() as ctx:
+        sb = ctx.enter_context(tc.tile_pool(name="sb", bufs=1))
+        psum = ctx.enter_context(tc.psum_pool(name="psum", bufs=1))
+
+        offsets = sb.tile([P, J // 16], U16)
+        nc.sync.dma_start(offsets[:], offs)
+
+        w_scale_raw = sb.tile([P, R], U8, align_bytes=64)
+        wb_scale = sb.tile([P, N], U8, align_bytes=64)
+        nc.gpsimd.memset(wb_scale[:].bitcast(I32), 0)
+
+        fk_sb = sb.tile([P, PACK], F32)
+        nc.scalar.dma_start(out=fk_sb[:], in_=fk.rearrange("(p t) o -> p (t o)", t=PACK))
+
+        load_scale_rows_repeated([nc.sync, nc.scalar, nc.scalar, nc.scalar], w_scale_raw, w_scales)
+        x_rows = xf.rearrange("(p t) c -> p t c", t=PACK)
+        x_front = sb.tile([P, 2 * T], F32)
+        nc.sync.dma_start(out=x_front[:], in_=x_rows[:, 0:2, :].rearrange("p t c -> p (t c)"))
+        x_planes = [x_front[:, 0:T], x_front[:, T : 2 * T]]
+        for t in range(2, PACK):
+            plane = sb.tile([P, T], F32, name=f"x_plane{t}")
+            nc.sync.dma_start(out=plane[:], in_=x_rows[:, t, :])
+            x_planes.append(plane[:])
+
+        w_raw = sb.tile([P, R], I32, align_bytes=64)
+        nc.sync.dma_start(out=w_raw[:], in_=w_words[0].rearrange("p c t -> p (c t)").bitcast(I32))
+        us_sb = sb.tile([P, PACK], F32)
+        nc.sync.dma_start(out=us_sb[:], in_=us.rearrange("(p t) o -> p (t o)", t=PACK))
+        wb_codes = sb.tile([P, 2 * N], U8, align_bytes=64)
+        nc.sync.dma_start(out=wb_codes[:].bitcast(I32), in_=wb_words[0].bitcast(I32))
+        rs_sb = sb.tile([P, N], F32)
+        load_scale_rows(nc.sync, wb_scale, wb_scales)
+        nc.sync.dma_start(out=rs_sb[:], in_=rs)
+
+        w_scale = sb.tile([P, R], U8, align_bytes=64)
+        nc.vector.tensor_copy(
+            out=w_scale[:].rearrange("p (t m) -> p t m", t=PACK),
+            in_=w_scale_raw[:].rearrange("p (m t) -> p t m", t=PACK),
+        )
+
+        fk_eighth = sb.tile([P, PACK], F32)
+        nc.scalar.activation(fk_eighth[:], fk_sb[:], ACT.Copy, scale=1.0 / GROUP)
+
+        u_grouped = sb.tile([P, J, PACK], BF16, align_bytes=64)
+        for first, count in ((0, 2), (2, 1), (3, 1)):
+            picked = sb.tile([P, count, J], F32, name=f"picked{first}")
+            for i in range(count):
+                window = x_planes[first + i].indirect(offsets[:])
+                nc.scalar.activation(picked[:, i, :], window, ACT.Copy)
+            by_group = picked[:].rearrange("p i (b e) -> p (i b) e", e=GROUP)
+            sums = sb.tile([P, count * B], F32, name=f"sums{first}")
+            nc.vector.tensor_reduce(out=sums[:], in_=by_group, axis=AXIS_X, op=ALU.add)
+            centred = sb.tile([P, count, J], F32, name=f"centred{first}")
+            nc.vector.scalar_tensor_tensor(
+                out=centred[:].rearrange("p i (b e) -> p (i b) e", e=GROUP), in0=by_group, scalar=float(GROUP),
+                in1=sums[:].unsqueeze(2).to_broadcast([P, count * B, GROUP]), op0=ALU.mult, op1=ALU.subtract,
+            )
+            for i in range(count):
+                t = first + i
+                nc.vector.tensor_scalar(
+                    out=u_grouped[:, :, t], in0=centred[:, i, :],
+                    scalar1=fk_eighth[:, t : t + 1], scalar2=None, op0=ALU.mult,
+                )
+
+        w_codes = sb.tile([P, R], I32, align_bytes=64)
+        nc.vector.tensor_copy(
+            out=w_codes[:].rearrange("p (t m) -> p m t", t=PACK),
+            in_=w_raw[:].rearrange("p (m t) -> p m t", t=PACK),
+        )
+
+        u_codes = sb.tile([P, J], U32, align_bytes=64)
+        u_scale = sb.tile([P, J], U8, align_bytes=64)
+        nc.vector.quantize_mx(out=u_codes[:].bitcast(E5M2X4), scales=u_scale[:], in_=u_grouped[:].rearrange("p j t -> p (j t)"))
+
+        peaks = sb.tile([P, PACK], F32)
+        a_sb = sb.tile([P, PACK, J], F32)
+        for t in range(PACK):
+            cols = slice(t * P, (t + 1) * P)
+            acc = psum.tile([P, J], F32, name=f"a_bank{t}")
+            nc.tensor.matmul_mx(
+                out=acc[:], lhsT=w_codes[:, cols].bitcast(E5M2X4), lhsT_scale=w_scale[:, cols],
+                rhs=u_codes[:].bitcast(E5M2X4), rhs_scale=u_scale[:], start=True, stop=True,
+            )
+            nc.scalar.activation(a_sb[:, t, :], acc[:], ACT.Copy)
+            nc.vector.tensor_reduce(out=peaks[:, t : t + 1], in_=a_sb[:, t, :], axis=AXIS_X, op=ALU.max, apply_absolute_value=True)
+
+        inv_peaks = sb.tile([P, PACK], F32)
+        nc.vector.reciprocal(out=inv_peaks[:], in_=peaks[:])
+        hid_grouped = sb.tile([P, J, PACK], BF16, align_bytes=64)
+        factor = sb.tile([P, PACK], F32)
+        nc.vector.tensor_tensor(out=factor[:], in0=inv_peaks[:], in1=us_sb[:], op=ALU.mult)
+        nc.vector.tensor_tensor(
+            out=hid_grouped[:].rearrange("p (c i) t -> p c t i", i=4),
+            in0=a_sb[:].rearrange("p t (c i) -> p c t i", i=4),
+            in1=factor[:].unsqueeze(1).unsqueeze(3).to_broadcast([P, J // 4, PACK, 4]),
+            op=ALU.mult,
+        )
+        hid_codes = sb.tile([P, J], U32, align_bytes=64)
+        hid_scale = sb.tile([P, J], U8, align_bytes=64)
+        nc.vector.quantize_mx(out=hid_codes[:].bitcast(E5M2X4), scales=hid_scale[:], in_=hid_grouped[:].rearrange("p j t -> p (j t)"))
+
+        rs_part = sb.tile([P, N], F32)
+        nc.gpsimd.tensor_scalar(out=rs_part[:], in0=rs_sb[:], scalar1=0.3, scalar2=0.0, op0=ALU.mult, op1=ALU.add)
+
+        prod = psum.tile([P, N], F32)
+        nc.tensor.matmul_mx(
+            out=prod[:], lhsT=hid_codes[:].bitcast(E5M2X4), lhsT_scale=hid_scale[:],
+            rhs=wb_codes[:].bitcast(E2M1X4), rhs_scale=wb_scale[:], start=True, stop=True,
+        )
+        magnitude = sb.tile([P, N], F32)
+        nc.scalar.activation(magnitude[:], prod[:], ACT.Abs)
+        shifted = sb.tile([P, N], F32)
+        denom = sb.tile([P, 1], F32)
+        nc.vector.tensor_scalar(
+            out=shifted[:], in0=magnitude[:], scalar1=0.2, scalar2=None, op0=ALU.add, op1=ALU.max, accum_out=denom[:],
+        )
+        inv_denom = sb.tile([P, 1], F32)
+        nc.vector.reciprocal(out=inv_denom[:], in_=denom[:])
+        result = sb.tile([P, N], F32)
+        nc.vector.scalar_tensor_tensor(
+            out=result[:], in0=prod[:], scalar=inv_denom[:], in1=rs_part[:], op0=ALU.mult, op1=ALU.add,
+        )
+        nc.sync.dma_start(out=out, in_=result[:])

@@ -52,18 +52,16 @@ def tile_list_centredpicks_peakscaled_rowpeaks_kernel(tc, xf, fk, w_words, w_sca
 
         w_scale_raw = sb.tile([P, R], U8, align_bytes=64)
         wb_scale = sb.tile([P, N], U8, align_bytes=64)
-        nc.gpsimd.memset(wb_scale[:].bitcast(I32), 0)
+        nc.vector.memset(wb_scale[:].bitcast(I32), 0)
 
         fk_sb = sb.tile([P, PACK], F32)
         nc.scalar.dma_start(out=fk_sb[:], in_=fk.rearrange("(p t) o -> p (t o)", t=PACK))
 
-        load_scale_rows_repeated([nc.sync, nc.scalar, nc.scalar, nc.scalar], w_scale_raw, w_scales)
+        load_scale_rows_repeated([nc.scalar, nc.scalar, nc.gpsimd, nc.gpsimd], w_scale_raw, w_scales)
         x_rows = xf.rearrange("(p t) c -> p t c", t=PACK)
-        x_front = sb.tile([P, 2 * T], F32)
-        nc.sync.dma_start(out=x_front[:], in_=x_rows[:, 0:2, :].rearrange("p t c -> p (t c)"))
-        x_planes = [x_front[:, 0:T], x_front[:, T : 2 * T]]
-        for t in range(2, PACK):
-            plane = sb.tile([P, T], F32, name=f"x_plane{t}")
+        x_planes = []
+        for t in range(PACK):
+            plane = sb.tile([P, T], F32, name=f"x_plane{t}", align_bytes=64, tag="u_then_w" if t == PACK - 1 else f"x_plane{t}")
             nc.sync.dma_start(out=plane[:], in_=x_rows[:, t, :])
             x_planes.append(plane[:])
 
@@ -78,7 +76,7 @@ def tile_list_centredpicks_peakscaled_rowpeaks_kernel(tc, xf, fk, w_words, w_sca
         nc.sync.dma_start(out=rs_sb[:], in_=rs)
 
         w_scale = sb.tile([P, R], U8, align_bytes=64)
-        nc.vector.tensor_copy(
+        nc.gpsimd.tensor_copy(
             out=w_scale[:].rearrange("p (t m) -> p t m", t=PACK),
             in_=w_scale_raw[:].rearrange("p (m t) -> p t m", t=PACK),
         )
@@ -86,8 +84,8 @@ def tile_list_centredpicks_peakscaled_rowpeaks_kernel(tc, xf, fk, w_words, w_sca
         fk_eighth = sb.tile([P, PACK], F32)
         nc.scalar.activation(fk_eighth[:], fk_sb[:], ACT.Copy, scale=1.0 / GROUP)
 
-        u_grouped = sb.tile([P, J, PACK], BF16, align_bytes=64)
-        for first, count in ((0, 2), (2, 1), (3, 1)):
+        centred_planes = []
+        for first, count in ((0, 1), (1, 1), (2, 1), (3, 1)):
             picked = sb.tile([P, count, J], F32, name=f"picked{first}")
             for i in range(count):
                 window = x_planes[first + i].indirect(offsets[:])
@@ -100,52 +98,57 @@ def tile_list_centredpicks_peakscaled_rowpeaks_kernel(tc, xf, fk, w_words, w_sca
                 out=centred[:].rearrange("p i (b e) -> p (i b) e", e=GROUP), in0=by_group, scalar=float(GROUP),
                 in1=sums[:].unsqueeze(2).to_broadcast([P, count * B, GROUP]), op0=ALU.mult, op1=ALU.subtract,
             )
-            for i in range(count):
-                t = first + i
+            centred_planes.append(centred)
+        u_grouped = sb.tile([P, J, PACK], BF16, align_bytes=64, tag="u_then_w")
+        for t in range(PACK):
+            if t < 2:
+                nc.scalar.activation(u_grouped[:, :, t], centred_planes[t][:, 0, :], ACT.Copy, scale=fk_eighth[:, t : t + 1])
+            else:
                 nc.vector.tensor_scalar(
-                    out=u_grouped[:, :, t], in0=centred[:, i, :],
+                    out=u_grouped[:, :, t], in0=centred_planes[t][:, 0, :],
                     scalar1=fk_eighth[:, t : t + 1], scalar2=None, op0=ALU.mult,
                 )
-
-        w_codes = sb.tile([P, R], I32, align_bytes=64)
-        nc.vector.tensor_copy(
-            out=w_codes[:].rearrange("p (t m) -> p m t", t=PACK),
-            in_=w_raw[:].rearrange("p (m t) -> p m t", t=PACK),
-        )
 
         u_codes = sb.tile([P, J], U32, align_bytes=64)
         u_scale = sb.tile([P, J], U8, align_bytes=64)
         nc.vector.quantize_mx(out=u_codes[:].bitcast(E5M2X4), scales=u_scale[:], in_=u_grouped[:].rearrange("p j t -> p (j t)"))
 
+        w_by_slot = w_raw[:].rearrange("p (m t) -> p t m", t=PACK)
         peaks = sb.tile([P, PACK], F32)
-        a_sb = sb.tile([P, PACK, J], F32)
+        a_abs = sb.tile([P, PACK, J], F32, tag="a_abs_then_rs")
+        banks = []
+        w_first = sb.tile([P, 2 * P], I32, align_bytes=64)
+        w_rest = sb.tile([P, 2 * P], I32, align_bytes=64, tag="u_then_w")
         for t in range(PACK):
-            cols = slice(t * P, (t + 1) * P)
+            w_codes = (w_first if t < 2 else w_rest)[:, (t % 2) * P : (t % 2 + 1) * P]
+            nc.vector.tensor_copy(out=w_codes, in_=w_by_slot[:, t, :])
             acc = psum.tile([P, J], F32, name=f"a_bank{t}")
             nc.tensor.matmul_mx(
-                out=acc[:], lhsT=w_codes[:, cols].bitcast(E5M2X4), lhsT_scale=w_scale[:, cols],
+                out=acc[:], lhsT=w_codes.bitcast(E5M2X4), lhsT_scale=w_scale[:, t * P : (t + 1) * P],
                 rhs=u_codes[:].bitcast(E5M2X4), rhs_scale=u_scale[:], start=True, stop=True,
             )
-            nc.scalar.activation(a_sb[:, t, :], acc[:], ACT.Copy)
-            nc.vector.tensor_reduce(out=peaks[:, t : t + 1], in_=a_sb[:, t, :], axis=AXIS_X, op=ALU.max, apply_absolute_value=True)
+            nc.scalar.activation(a_abs[:, t, :], acc[:], ACT.Abs)
+            nc.vector.tensor_reduce(out=peaks[:, t : t + 1], in_=a_abs[:, t, :], axis=AXIS_X, op=ALU.max)
+            banks.append(acc)
 
+        a_us = sb.tile([P, PACK, J], F32)
+        for t in range(PACK):
+            nc.scalar.activation(a_us[:, t, :], banks[t][:], ACT.Copy, scale=us_sb[:, t : t + 1])
         inv_peaks = sb.tile([P, PACK], F32)
         nc.vector.reciprocal(out=inv_peaks[:], in_=peaks[:])
         hid_grouped = sb.tile([P, J, PACK], BF16, align_bytes=64)
-        factor = sb.tile([P, PACK], F32)
-        nc.vector.tensor_tensor(out=factor[:], in0=inv_peaks[:], in1=us_sb[:], op=ALU.mult)
         nc.vector.tensor_tensor(
-            out=hid_grouped[:].rearrange("p (c i) t -> p c t i", i=4),
-            in0=a_sb[:].rearrange("p t (c i) -> p c t i", i=4),
-            in1=factor[:].unsqueeze(1).unsqueeze(3).to_broadcast([P, J // 4, PACK, 4]),
+            out=hid_grouped[:].rearrange("p (c i) t -> p c t i", i=2),
+            in0=a_us[:].rearrange("p t (c i) -> p c t i", i=2),
+            in1=inv_peaks[:].unsqueeze(1).unsqueeze(3).to_broadcast([P, J // 2, PACK, 2]),
             op=ALU.mult,
         )
         hid_codes = sb.tile([P, J], U32, align_bytes=64)
         hid_scale = sb.tile([P, J], U8, align_bytes=64)
         nc.vector.quantize_mx(out=hid_codes[:].bitcast(E5M2X4), scales=hid_scale[:], in_=hid_grouped[:].rearrange("p j t -> p (j t)"))
 
-        rs_part = sb.tile([P, N], F32)
-        nc.gpsimd.tensor_scalar(out=rs_part[:], in0=rs_sb[:], scalar1=0.3, scalar2=0.0, op0=ALU.mult, op1=ALU.add)
+        rs_part = sb.tile([P, N], F32, tag="a_abs_then_rs")
+        nc.scalar.activation(rs_part[:], rs_sb[:], ACT.Copy, scale=0.3)
 
         prod = psum.tile([P, N], F32)
         nc.tensor.matmul_mx(
@@ -161,8 +164,10 @@ def tile_list_centredpicks_peakscaled_rowpeaks_kernel(tc, xf, fk, w_words, w_sca
         )
         inv_denom = sb.tile([P, 1], F32)
         nc.vector.reciprocal(out=inv_denom[:], in_=denom[:])
-        result = sb.tile([P, N], F32)
-        nc.vector.scalar_tensor_tensor(
-            out=result[:], in0=prod[:], scalar=inv_denom[:], in1=rs_part[:], op0=ALU.mult, op1=ALU.add,
-        )
-        nc.sync.dma_start(out=out, in_=result[:])
+        for h, queue in enumerate((nc.scalar, nc.sync)):
+            cols = slice(h * N // 2, (h + 1) * N // 2)
+            result = sb.tile([P, N // 2], F32, name=f"result{h}")
+            nc.vector.scalar_tensor_tensor(
+                out=result[:], in0=prod[:, cols], scalar=inv_denom[:], in1=rs_part[:, cols], op0=ALU.mult, op1=ALU.add,
+            )
+            queue.dma_start(out=out[:, cols], in_=result[:])

@@ -54,17 +54,19 @@ def tile_list_centredpicks_peakscaled_rowpeaks_kernel(tc, xf, fk, w_words, w_sca
         wb_scale = sb.tile([P, N], U8, align_bytes=64)
         nc.vector.memset(wb_scale[:].bitcast(I32), 0)
 
-        fk_sb = sb.tile([P, PACK], F32)
-        nc.scalar.dma_start(out=fk_sb[:], in_=fk.rearrange("(p t) o -> p (t o)", t=PACK))
 
-        load_scale_rows_repeated([nc.scalar, nc.scalar, nc.gpsimd, nc.gpsimd], w_scale_raw, w_scales)
+        load_scale_rows_repeated([nc.scalar] * QUADRANTS, w_scale_raw, w_scales)
         x_rows = xf.rearrange("(p t) c -> p t c", t=PACK)
-        x_planes = []
-        for t in range(PACK):
+        x_front = sb.tile([P, 2 * T], F32)
+        nc.sync.dma_start(out=x_front[:], in_=x_rows[:, 0:2, :].rearrange("p t c -> p (t c)"))
+        x_planes = [x_front[:, 0:T], x_front[:, T : 2 * T]]
+        for t in range(2, PACK):
             plane = sb.tile([P, T], F32, name=f"x_plane{t}", align_bytes=64, tag="u_then_w" if t == PACK - 1 else f"x_plane{t}")
             nc.sync.dma_start(out=plane[:], in_=x_rows[:, t, :])
             x_planes.append(plane[:])
 
+        fk_sb = sb.tile([P, PACK], F32)
+        nc.sync.dma_start(out=fk_sb[:], in_=fk.rearrange("(p t) o -> p (t o)", t=PACK))
         w_raw = sb.tile([P, R], I32, align_bytes=64)
         nc.sync.dma_start(out=w_raw[:], in_=w_words[0].rearrange("p c t -> p (c t)").bitcast(I32))
         us_sb = sb.tile([P, PACK], F32)
@@ -81,39 +83,44 @@ def tile_list_centredpicks_peakscaled_rowpeaks_kernel(tc, xf, fk, w_words, w_sca
             in_=w_scale_raw[:].rearrange("p (m t) -> p t m", t=PACK),
         )
 
-        fk_eighth = sb.tile([P, PACK], F32)
-        nc.scalar.activation(fk_eighth[:], fk_sb[:], ACT.Copy, scale=1.0 / GROUP)
+        warm_in = sb.tile([P, 1], F32)
+        nc.vector.memset(warm_in[:], 0.0)
+        warm_out = sb.tile([P, 1], F32)
+        nc.scalar.activation(warm_out[:], warm_in[:], ACT.Copy)
 
         centred_planes = []
-        for first, count in ((0, 1), (1, 1), (2, 1), (3, 1)):
+        for first, count in ((0, 2), (2, 1), (3, 1)):
             picked = sb.tile([P, count, J], F32, name=f"picked{first}")
             for i in range(count):
                 window = x_planes[first + i].indirect(offsets[:])
-                nc.scalar.activation(picked[:, i, :], window, ACT.Copy)
+                if first + i == 1:
+                    nc.vector.tensor_copy(out=picked[:, i, :], in_=window)
+                else:
+                    nc.scalar.activation(picked[:, i, :], window, ACT.Copy)
             by_group = picked[:].rearrange("p i (b e) -> p (i b) e", e=GROUP)
             sums = sb.tile([P, count * B], F32, name=f"sums{first}")
             nc.vector.tensor_reduce(out=sums[:], in_=by_group, axis=AXIS_X, op=ALU.add)
             centred = sb.tile([P, count, J], F32, name=f"centred{first}")
             nc.vector.scalar_tensor_tensor(
-                out=centred[:].rearrange("p i (b e) -> p (i b) e", e=GROUP), in0=by_group, scalar=float(GROUP),
-                in1=sums[:].unsqueeze(2).to_broadcast([P, count * B, GROUP]), op0=ALU.mult, op1=ALU.subtract,
+                out=centred[:].rearrange("p i (b e) -> p (i b) e", e=GROUP), in1=by_group, scalar=-1.0 / GROUP,
+                in0=sums[:].unsqueeze(2).to_broadcast([P, count * B, GROUP]), op0=ALU.mult, op1=ALU.add,
             )
-            centred_planes.append(centred)
+            centred_planes.extend([centred[:, i, :] for i in range(count)])
         u_grouped = sb.tile([P, J, PACK], BF16, align_bytes=64, tag="u_then_w")
         for t in range(PACK):
             if t < 2:
-                nc.scalar.activation(u_grouped[:, :, t], centred_planes[t][:, 0, :], ACT.Copy, scale=fk_eighth[:, t : t + 1])
+                nc.scalar.activation(u_grouped[:, :, t], centred_planes[t], ACT.Copy, scale=fk_sb[:, t : t + 1])
             else:
                 nc.vector.tensor_scalar(
-                    out=u_grouped[:, :, t], in0=centred_planes[t][:, 0, :],
-                    scalar1=fk_eighth[:, t : t + 1], scalar2=None, op0=ALU.mult,
+                    out=u_grouped[:, :, t], in0=centred_planes[t],
+                    scalar1=fk_sb[:, t : t + 1], scalar2=None, op0=ALU.mult,
                 )
 
         u_codes = sb.tile([P, J], U32, align_bytes=64)
         u_scale = sb.tile([P, J], U8, align_bytes=64)
         nc.vector.quantize_mx(out=u_codes[:].bitcast(E5M2X4), scales=u_scale[:], in_=u_grouped[:].rearrange("p j t -> p (j t)"))
 
-        w_by_slot = w_raw[:].rearrange("p (m t) -> p t m", t=PACK)
+        w_by_slot = w_raw[:].rearrange("p (m t) -> p m t", t=PACK)
         peaks = sb.tile([P, PACK], F32)
         a_abs = sb.tile([P, PACK, J], F32, tag="a_abs_then_rs")
         banks = []
@@ -121,7 +128,10 @@ def tile_list_centredpicks_peakscaled_rowpeaks_kernel(tc, xf, fk, w_words, w_sca
         w_rest = sb.tile([P, 2 * P], I32, align_bytes=64, tag="u_then_w")
         for t in range(PACK):
             w_codes = (w_first if t < 2 else w_rest)[:, (t % 2) * P : (t % 2 + 1) * P]
-            nc.vector.tensor_copy(out=w_codes, in_=w_by_slot[:, t, :])
+            if t % 2 == 0:
+                nc.vector.tensor_copy(
+                    out=(w_first if t < 2 else w_rest)[:].rearrange("p (t m) -> p m t", t=2), in_=w_by_slot[:, :, t : t + 2],
+                )
             acc = psum.tile([P, J], F32, name=f"a_bank{t}")
             nc.tensor.matmul_mx(
                 out=acc[:], lhsT=w_codes.bitcast(E5M2X4), lhsT_scale=w_scale[:, t * P : (t + 1) * P],
@@ -150,13 +160,17 @@ def tile_list_centredpicks_peakscaled_rowpeaks_kernel(tc, xf, fk, w_words, w_sca
         rs_part = sb.tile([P, N], F32, tag="a_abs_then_rs")
         nc.scalar.activation(rs_part[:], rs_sb[:], ACT.Copy, scale=0.3)
 
-        prod = psum.tile([P, N], F32)
-        nc.tensor.matmul_mx(
-            out=prod[:], lhsT=hid_codes[:].bitcast(E5M2X4), lhsT_scale=hid_scale[:],
-            rhs=wb_codes[:].bitcast(E2M1X4), rhs_scale=wb_scale[:], start=True, stop=True,
-        )
         magnitude = sb.tile([P, N], F32)
-        nc.scalar.activation(magnitude[:], prod[:], ACT.Abs)
+        prods = []
+        for h in range(2):
+            cols = slice(h * N // 2, (h + 1) * N // 2)
+            prod = psum.tile([P, N // 2], F32, name=f"prod{h}")
+            nc.tensor.matmul_mx(
+                out=prod[:], lhsT=hid_codes[:].bitcast(E5M2X4), lhsT_scale=hid_scale[:],
+                rhs=wb_codes[:, h * N : (h + 1) * N].bitcast(E2M1X4), rhs_scale=wb_scale[:, cols], start=True, stop=True,
+            )
+            nc.scalar.activation(magnitude[:, cols], prod[:], ACT.Abs)
+            prods.append(prod)
         shifted = sb.tile([P, N], F32)
         denom = sb.tile([P, 1], F32)
         nc.vector.tensor_scalar(
@@ -168,6 +182,6 @@ def tile_list_centredpicks_peakscaled_rowpeaks_kernel(tc, xf, fk, w_words, w_sca
             cols = slice(h * N // 2, (h + 1) * N // 2)
             result = sb.tile([P, N // 2], F32, name=f"result{h}")
             nc.vector.scalar_tensor_tensor(
-                out=result[:], in0=prod[:, cols], scalar=inv_denom[:], in1=rs_part[:, cols], op0=ALU.mult, op1=ALU.add,
+                out=result[:], in0=prods[h][:], scalar=inv_denom[:], in1=rs_part[:, cols], op0=ALU.mult, op1=ALU.add,
             )
             queue.dma_start(out=out[:, cols], in_=result[:])

from contextlib import ExitStack

import concourse.mybir as mybir

K, T, J, B, R, N = 512, 512, 128, 16, 512, 256
FLOPS = 2 * K * R * J + 2 * R * J * N

F32 = mybir.dt.float32
BF16 = mybir.dt.bfloat16
I32 = mybir.dt.int32
U32 = mybir.dt.uint32
U16 = mybir.dt.uint16
U8 = mybir.dt.uint8
E5M2X4 = mybir.dt.float8_e5m2_x4
E2M1X4 = mybir.dt.float4_e2m1fn_x4
ALU = mybir.AluOpType
ACT = mybir.ActivationFunctionType
AXIS_X = mybir.AxisListType.X

P = 128
PACK = 4
GROUP = J // B
QUADRANTS = 4


def load_scale_rows(queue, plane, scales):
    rows = scales[0].bitcast(I32)
    view = plane[:].bitcast(I32)
    for q in range(QUADRANTS):
        queue.dma_start(out=view[32 * q : 32 * q + 4, :], in_=rows[4 * q : 4 * q + 4, :])


def load_scale_rows_repeated(queues, plane, scales):
    rows = scales[0].bitcast(I32)
    view = plane[:].bitcast(I32)
    words = rows.shape[1]
    for q in range(QUADRANTS):
        queues[q].dma_start(
            out=view[32 * q : 32 * q + 32, :],
            in_=rows[4 * q : 4 * q + 4, :].unsqueeze(0).to_broadcast([8, 4, words]),
        )


def tile_list_centredpicks_peakscaled_rowpeaks_kernel(tc, xf, fk, w_words, w_scales, us, wb_words, wb_scales, rs, offs, out):
    nc = tc.nc
    with ExitStack() as ctx:
        sb = ctx.enter_context(tc.tile_pool(name="sb", bufs=1))
        psum = ctx.enter_context(tc.psum_pool(name="psum", bufs=1))

        offsets = sb.tile([P, J // 16], U16)
        nc.sync.dma_start(offsets[:], offs)

        w_scale_raw = sb.tile([P, R], U8, align_bytes=64)
        wb_scale = sb.tile([P, N], U8, align_bytes=64)
        nc.vector.memset(wb_scale[:].bitcast(I32), 0)


        load_scale_rows_repeated([nc.scalar] * QUADRANTS, w_scale_raw, w_scales)
        x_rows = xf.rearrange("(p t) c -> p t c", t=PACK)
        x_front = sb.tile([P, 2 * T], F32)
        nc.sync.dma_start(out=x_front[:], in_=x_rows[:, 0:2, :].rearrange("p t c -> p (t c)"))
        x_planes = [x_front[:, 0:T], x_front[:, T : 2 * T]]
        for t in range(2, PACK):
            plane = sb.tile([P, T], F32, name=f"x_plane{t}", align_bytes=64, tag="u_then_w" if t == PACK - 1 else f"x_plane{t}")
            nc.sync.dma_start(out=plane[:], in_=x_rows[:, t, :])
            x_planes.append(plane[:])

        fk_sb = sb.tile([P, PACK], F32)
        nc.sync.dma_start(out=fk_sb[:], in_=fk.rearrange("(p t) o -> p (t o)", t=PACK))
        w_raw = sb.tile([P, R], I32, align_bytes=64)
        nc.sync.dma_start(out=w_raw[:], in_=w_words[0].rearrange("p c t -> p (c t)").bitcast(I32))
        us_sb = sb.tile([P, PACK], F32)
        nc.sync.dma_start(out=us_sb[:], in_=us.rearrange("(p t) o -> p (t o)", t=PACK))
        wb_codes = sb.tile([P, 2 * N], U8, align_bytes=64)
        nc.sync.dma_start(out=wb_codes[:].bitcast(I32), in_=wb_words[0].bitcast(I32))
        rs_sb = sb.tile([P, N], F32)
        load_scale_rows(nc.sync, wb_scale, wb_scales)
        nc.sync.dma_start(out=rs_sb[:], in_=rs)

        w_scale = sb.tile([P, R], U8, align_bytes=64)
        nc.gpsimd.tensor_copy(
            out=w_scale[:].rearrange("p (t m) -> p t m", t=PACK),
            in_=w_scale_raw[:].rearrange("p (m t) -> p t m", t=PACK),
        )

        warm_in = sb.tile([P, 1], F32)
        nc.vector.memset(warm_in[:], 0.0)
        warm_out = sb.tile([P, 1], F32)
        nc.scalar.activation(warm_out[:], warm_in[:], ACT.Copy)

        centred_planes = []
        for first, count in ((0, 2), (2, 1), (3, 1)):
            picked = sb.tile([P, count, J], F32, name=f"picked{first}")
            for i in range(count):
                window = x_planes[first + i].indirect(offsets[:])
                if first + i == 1:
                    nc.vector.tensor_copy(out=picked[:, i, :], in_=window)
                else:
                    nc.scalar.activation(picked[:, i, :], window, ACT.Copy)
            by_group = picked[:].rearrange("p i (b e) -> p (i b) e", e=GROUP)
            sums = sb.tile([P, count * B], F32, name=f"sums{first}")
            nc.vector.tensor_reduce(out=sums[:], in_=by_group, axis=AXIS_X, op=ALU.add)
            centred = sb.tile([P, count, J], F32, name=f"centred{first}")
            nc.vector.scalar_tensor_tensor(
                out=centred[:].rearrange("p i (b e) -> p (i b) e", e=GROUP), in1=by_group, scalar=-1.0 / GROUP,
                in0=sums[:].unsqueeze(2).to_broadcast([P, count * B, GROUP]), op0=ALU.mult, op1=ALU.add,
            )
            centred_planes.extend([centred[:, i, :] for i in range(count)])
        u_grouped = sb.tile([P, J, PACK], BF16, align_bytes=64, tag="u_then_w")
        for t in range(PACK):
            if t < 2:
                nc.scalar.activation(u_grouped[:, :, t], centred_planes[t], ACT.Copy, scale=fk_sb[:, t : t + 1])
            else:
                nc.vector.tensor_scalar(
                    out=u_grouped[:, :, t], in0=centred_planes[t],
                    scalar1=fk_sb[:, t : t + 1], scalar2=None, op0=ALU.mult,
                )

        u_codes = sb.tile([P, J], U32, align_bytes=64)
        u_scale = sb.tile([P, J], U8, align_bytes=64)
        nc.vector.quantize_mx(out=u_codes[:].bitcast(E5M2X4), scales=u_scale[:], in_=u_grouped[:].rearrange("p j t -> p (j t)"))

        w_by_slot = w_raw[:].rearrange("p (m t) -> p m t", t=PACK)
        peaks = sb.tile([P, PACK], F32)
        a_abs = sb.tile([P, PACK, J], F32, tag="a_abs_then_rs")
        banks = []
        w_first = sb.tile([P, 2 * P], I32, align_bytes=64)
        w_rest = sb.tile([P, 2 * P], I32, align_bytes=64, tag="u_then_w")
        for t in range(PACK):
            w_codes = (w_first if t < 2 else w_rest)[:, (t % 2) * P : (t % 2 + 1) * P]
            if t % 2 == 0:
                nc.vector.tensor_copy(
                    out=(w_first if t < 2 else w_rest)[:].rearrange("p (t m) -> p m t", t=2), in_=w_by_slot[:, :, t : t + 2],
                )
            acc = psum.tile([P, J], F32, name=f"a_bank{t}")
            nc.tensor.matmul_mx(
                out=acc[:], lhsT=w_codes.bitcast(E5M2X4), lhsT_scale=w_scale[:, t * P : (t + 1) * P],
                rhs=u_codes[:].bitcast(E5M2X4), rhs_scale=u_scale[:], start=True, stop=True,
            )
            nc.scalar.activation(a_abs[:, t, :], acc[:], ACT.Abs)
            nc.vector.tensor_reduce(out=peaks[:, t : t + 1], in_=a_abs[:, t, :], axis=AXIS_X, op=ALU.max)
            banks.append(acc)

        a_us = sb.tile([P, PACK, J], F32)
        for t in range(PACK):
            nc.scalar.activation(a_us[:, t, :], banks[t][:], ACT.Copy, scale=us_sb[:, t : t + 1])
        inv_peaks = sb.tile([P, PACK], F32)
        nc.vector.reciprocal(out=inv_peaks[:], in_=peaks[:])
        hid_grouped = sb.tile([P, J, PACK], BF16, align_bytes=64)
        nc.vector.tensor_tensor(
            out=hid_grouped[:].rearrange("p (c i) t -> p c t i", i=2),
            in0=a_us[:].rearrange("p t (c i) -> p c t i", i=2),
            in1=inv_peaks[:].unsqueeze(1).unsqueeze(3).to_broadcast([P, J // 2, PACK, 2]),
            op=ALU.mult,
        )
        hid_codes = sb.tile([P, J], U32, align_bytes=64)
        hid_scale = sb.tile([P, J], U8, align_bytes=64)
        nc.vector.quantize_mx(out=hid_codes[:].bitcast(E5M2X4), scales=hid_scale[:], in_=hid_grouped[:].rearrange("p j t -> p (j t)"))

        rs_part = sb.tile([P, N], F32, tag="a_abs_then_rs")
        nc.scalar.activation(rs_part[:], rs_sb[:], ACT.Copy, scale=0.3)

        magnitude = sb.tile([P, N], F32)
        prods = []
        for h in range(2):
            cols = slice(h * N // 2, (h + 1) * N // 2)
            prod = psum.tile([P, N // 2], F32, name=f"prod{h}")
            nc.tensor.matmul_mx(
                out=prod[:], lhsT=hid_codes[:].bitcast(E5M2X4), lhsT_scale=hid_scale[:],
                rhs=wb_codes[:, h * N : (h + 1) * N].bitcast(E2M1X4), rhs_scale=wb_scale[:, cols], start=True, stop=True,
            )
            nc.scalar.activation(magnitude[:, cols], prod[:], ACT.Abs)
            prods.append(prod)
        shifted = sb.tile([P, N], F32)
        denom = sb.tile([P, 1], F32)
        nc.vector.tensor_scalar(
            out=shifted[:], in0=magnitude[:], scalar1=0.2, scalar2=None, op0=ALU.add, op1=ALU.max, accum_out=denom[:],
        )
        inv_denom = sb.tile([P, 1], F32)
        nc.vector.reciprocal(out=inv_denom[:], in_=denom[:])
        for h, queue in enumerate((nc.scalar, nc.sync)):
            cols = slice(h * N // 2, (h + 1) * N // 2)
            result = sb.tile([P, N // 2], F32, name=f"result{h}")
            nc.vector.scalar_tensor_tensor(
                out=result[:], in0=prods[h][:], scalar=inv_denom[:], in1=rs_part[:, cols], op0=ALU.mult, op1=ALU.add,
            )
            queue.dma_start(out=out[:, cols], in_=result[:])
